import numpy as np
import ml_dtypes


def mxq(x, axis, fmt="e4m3"):
    dtype, down = {"e4m3": (ml_dtypes.float8_e4m3fn, 7), "e5m2": (ml_dtypes.float8_e5m2, 14)}[fmt]
    v = np.moveaxis(np.asarray(x, np.float32).astype(ml_dtypes.bfloat16).astype(np.float64), axis, -1)
    blocks = v.reshape(v.shape[:-1] + (-1, 32))
    amax = np.abs(blocks).max(-1, keepdims=True)
    byte = np.maximum(np.where(amax > 0, np.frexp(amax)[1] - 1 + 127, 0) - down, 1)
    scale = np.exp2(byte - 127.0)
    codes = (blocks / scale).astype(np.float32).astype(dtype).astype(np.float64)
    return np.moveaxis((codes * scale).reshape(v.shape), -1, axis)


WIDE = False


def mx_kscale(k):
    if not WIDE:
        return np.ones(k)
    levels = np.array([30, -30])
    if k % 512:
        return np.exp2(np.random.permutation(np.resize(levels, k // 32))).repeat(32)
    a = np.empty((k // 512, 16))
    for p in range(k // 512):
        a[p, :8] = np.random.permutation(np.resize(levels, 8))
        for g in range(8):
            far = levels[np.abs(levels - a[p, g]) >= 10]
            a[p, g + 8] = far[np.random.randint(len(far))]
    return np.exp2(a.ravel()).repeat(32)


def f64(x):
    return np.asarray(x).astype(np.float64)


def striped(idx):
    return np.tile(np.asarray(idx).reshape(-1, 16).T, (8, 1)).astype(np.uint16)


def unstriped(offs):
    return offs[:16].T.reshape(-1).astype(np.int64)


E2M1 = np.array([0.0, 0.5, 1.0, 1.5, 2.0, 3.0, 4.0, 6.0, -0.0, -0.5, -1.0, -1.5, -2.0, -3.0, -4.0, -6.0])


def pack_weight(w, fmt):
    k, n = w.shape
    w = f64(np.asarray(w, np.float32).astype(ml_dtypes.bfloat16)).reshape(k // 32, 32, n)
    amax = np.abs(w).max(1)
    if fmt in ("e4m3", "e5m2"):
        byte = np.frexp(amax)[1] - 1 + 127 - (7 if fmt == "e4m3" else 14)
    else:
        mant, ex = np.frexp(amax / 6.0)
        byte = np.where(mant > 0.5, ex, ex - 1) + 127
    byte = np.clip(np.where(amax > 0, byte, 1), 1, 254)
    scaled = (w * np.exp2(127.0 - byte)[:, None, :]).reshape(k, n).astype(np.float32)
    by_word = np.ascontiguousarray(scaled.reshape(k // 512, 128, 4, n).transpose(0, 1, 3, 2))
    if fmt in ("e4m3", "e5m2"):
        words = by_word.astype(ml_dtypes.float8_e4m3fn if fmt == "e4m3" else ml_dtypes.float8_e5m2).view(np.uint8)
    else:
        c = by_word.astype(ml_dtypes.float4_e2m1fn).view(np.uint8) & 0xF
        words = (c[..., 0::2] | (c[..., 1::2] << 4)).reshape(k // 512, 128, 2 * n)
    return np.ascontiguousarray(words), np.ascontiguousarray(byte.astype(np.uint8).reshape(k // 512, 16, n))


def unpack_weight(words, scales, fmt):
    g, _, n = scales.shape
    words = np.ascontiguousarray(words).reshape(g, 128, n, -1)
    if fmt in ("e4m3", "e5m2"):
        vals = words.view(ml_dtypes.float8_e4m3fn if fmt == "e4m3" else ml_dtypes.float8_e5m2).astype(np.float64)
    else:
        nib = np.empty((g, 128, n, 4), np.uint8)
        nib[..., 0::2] = words & 0xF
        nib[..., 1::2] = words >> 4
        vals = E2M1[nib]
    vals = vals * np.repeat(np.exp2(scales.astype(np.float64) - 127.0), 8, axis=1)[..., None]
    return vals.transpose(0, 1, 3, 2).reshape(g * 512, n)


K, T, J, R, V, N = 512, 1024, 256, 512, 1024, 256


def setup_inputs():
    n = np.random.standard_normal
    idx = np.random.permutation(T)[:J]
    idx2 = np.random.permutation(V)[:J]
    idx3 = np.random.permutation(V)[:J]
    idx4 = np.random.permutation(T)[:J]
    fk = mx_kscale(K)
    fr = mx_kscale(R)
    xtp = pack_weight(n((K, T)) / fk[:, None], "e5m2")
    wp = pack_weight(n((K, R)) * 1 / np.sqrt(K) * fk[:, None] * fr, "e2m1")
    wbp = pack_weight(n((R, N)) * 1 / np.sqrt(R) / fr[:, None], "e2m1")
    wsp = pack_weight(n((K, N)) * 1 / np.sqrt(K) * fk[:, None], "e2m1")
    return {
        "xt_words": xtp[0],
        "xt_scales": xtp[1],
        "w_words": wp[0],
        "w_scales": wp[1],
        "tb": (np.random.randint(-9, 10, (R, V)).astype(np.float64)).astype(np.float32),
        "sa": (np.random.uniform(0.12, 0.3, (R, 1)) * fr[:, None]).astype(np.float32),
        "sb": (np.random.uniform(0.06, 0.2, (R, 1)) * fr[:, None]).astype(np.float32),
        "wb_words": wbp[0],
        "wb_scales": wbp[1],
        "ws_words": wsp[0],
        "ws_scales": wsp[1],
        "offs": striped(idx),
        "offs2": striped(idx2),
        "offs3": striped(idx3),
        "offs4": striped(idx4),
    }


def reference(xt_words, xt_scales, w_words, w_scales, tb, sa, sb, wb_words, wb_scales, ws_words, ws_scales, offs, offs2, offs3, offs4):
    idx = unstriped(offs)
    idx2 = unstriped(offs2)
    idx3 = unstriped(offs3)
    idx4 = unstriped(offs4)
    xtu = unpack_weight(xt_words, xt_scales, "e5m2")
    wu = unpack_weight(w_words, w_scales, "e2m1")
    wbu = unpack_weight(wb_words, wb_scales, "e2m1")
    wsu = unpack_weight(ws_words, ws_scales, "e2m1")
    xtidxg = xtu[:, idx]
    a = wu.T @ xtidxg
    hid = np.maximum(np.minimum(a, f64(tb)[:, idx2] * f64(sa)), f64(tb)[:, idx3] * f64(sb))
    hidq = mxq(hid, 0, "e4m3")
    xtidx4g = xtu[:, idx4]
    y = wbu.T @ hidq + wsu.T @ xtidx4g
    return y

@@ -1,0 +1,193 @@
+from contextlib import ExitStack
+
+import concourse.mybir as mybir
+
+K, T, J, R, V, N = 512, 1024, 256, 512, 1024, 256
+FLOPS = 2 * K * R * J + 2 * R * N * J + 2 * K * N * J
+
+F32 = mybir.dt.float32
+BF16 = mybir.dt.bfloat16
+I32 = mybir.dt.int32
+U32 = mybir.dt.uint32
+U16 = mybir.dt.uint16
+U8 = mybir.dt.uint8
+E4M3X4 = mybir.dt.float8_e4m3fn_x4
+E5M2X4 = mybir.dt.float8_e5m2_x4
+E2M1X4 = mybir.dt.float4_e2m1fn_x4
+COPY = mybir.ActivationFunctionType.Copy
+MIN = mybir.AluOpType.min
+MAX = mybir.AluOpType.max
+
+P = 128
+PACK = 4
+QUADS = 4
+QUAD = 32
+ROWS = 4
+HALF = J // 2
+LIST_COLS = J // 16
+
+
+def load_scale_rows(queue, staged, scales):
+    queue.dma_start(out=staged, in_=scales[0].rearrange("(q r) c -> r q c", r=ROWS).bitcast(I32))
+
+
+def tile_list_twostepbounds_solo_further_plain_kernel(
+    tc, xt_words, xt_scales, w_words, w_scales, tb, sa, sb, wb_words, wb_scales, ws_words, ws_scales,
+    offs, offs2, offs3, offs4, out,
+):
+    nc = tc.nc
+    with ExitStack() as ctx:
+        keep = ctx.enter_context(tc.tile_pool(name="keep", bufs=1))
+        psum = ctx.enter_context(tc.psum_pool(name="psum", bufs=1))
+
+        idx = keep.tile([P, LIST_COLS], U16, name="idx")
+        idx2 = keep.tile([P, LIST_COLS], U16, name="idx2")
+        idx3 = keep.tile([P, LIST_COLS], U16, name="idx3")
+        idx4 = keep.tile([P, LIST_COLS], U16, name="idx4")
+        table = [keep.tile([P, V], F32, name=f"table{t}", align_bytes=64) for t in range(PACK)]
+        upper_step = keep.tile([P, PACK], F32, name="upper_step")
+        lower_step = keep.tile([P, PACK], F32, name="lower_step")
+        x_words = keep.tile([P, T], I32, name="x_words", align_bytes=64)
+        x_staged = keep.tile([ROWS, QUADS, T // 4], I32, name="x_staged")
+        x_plane = keep.tile([P, T], U8, name="x_plane", align_bytes=64)
+        w_raw = keep.tile([P, R // 2], I32, name="w_raw", align_bytes=64)
+        w_staged = keep.tile([ROWS, QUADS, R // 4], I32, name="w_staged")
+        w_plane_raw = keep.tile([P, R], U8, name="w_plane_raw", align_bytes=64)
+        w_dealt = keep.tile([P, R], U16, name="w_dealt", align_bytes=64)
+        w_plane = keep.tile([P, R], U8, name="w_plane", align_bytes=64)
+        ws_codes = keep.tile([P, 2 * N], U8, name="ws_codes", align_bytes=64)
+        wb_codes = keep.tile([P, 2 * N], U8, name="wb_codes", align_bytes=64)
+        out_staged = keep.tile([ROWS, 2, QUADS, N // 4], I32, name="out_staged")
+        out_plane = keep.tile([P, 2 * N], U8, name="out_plane", align_bytes=64)
+
+        tb_planes = tb.rearrange("(p t) v -> p t v", t=PACK)
+
+        nc.sync.dma_start(idx2[:], offs2)
+        nc.sync.dma_start(out=upper_step[:], in_=sa.rearrange("(p t) o -> p (t o)", t=PACK))
+        nc.sync.dma_start(out=table[0][:], in_=tb_planes[:, 0, :])
+        load_scale_rows(nc.sync, x_staged[:], xt_scales)
+        nc.sync.dma_start(idx3[:], offs3)
+        nc.sync.dma_start(out=lower_step[:], in_=sb.rearrange("(p t) o -> p (t o)", t=PACK))
+        nc.sync.dma_start(idx[:], offs)
+        nc.sync.dma_start(out=table[1][:], in_=tb_planes[:, 1, :])
+        load_scale_rows(nc.sync, w_staged[:], w_scales)
+        nc.sync.dma_start(out=x_words[:], in_=xt_words[0].rearrange("p c r -> p (c r)").bitcast(I32))
+        nc.sync.dma_start(out=w_raw[:], in_=w_words[0].bitcast(I32))
+        nc.sync.dma_start(idx4[:], offs4)
+        nc.sync.dma_start(out=table[2][:], in_=tb_planes[:, 2, :])
+        load_scale_rows(nc.sync, out_staged[:, 0, :, :], ws_scales)
+        load_scale_rows(nc.sync, out_staged[:, 1, :, :], wb_scales)
+        nc.sync.dma_start(out=table[3][:], in_=tb_planes[:, 3, :])
+        nc.sync.dma_start(out=ws_codes[:].bitcast(I32), in_=ws_words[0].bitcast(I32))
+        nc.sync.dma_start(out=wb_codes[:].bitcast(I32), in_=wb_words[0].bitcast(I32))
+
+        nc.vector.memset(x_plane[:].bitcast(I32), 0)
+        nc.vector.memset(w_plane_raw[:].bitcast(I32), 0)
+        nc.vector.memset(out_plane[:].bitcast(I32), 0)
+        for q in range(QUADS):
+            rows = slice(QUAD * q, QUAD * q + ROWS)
+            nc.vector.tensor_copy(out=x_plane[rows, :].bitcast(I32), in_=x_staged[:, q, :])
+        for q in range(QUADS):
+            rows = slice(QUAD * q, QUAD * q + ROWS)
+            nc.vector.tensor_copy(out=w_plane_raw[rows, :].bitcast(I32), in_=w_staged[:, q, :])
+
+        x_picked_plane = keep.tile([P, J], U8, name="x_picked_plane", align_bytes=64)
+        nc.vector.tensor_copy(x_picked_plane[:], x_plane[:].indirect(idx[:]))
+        nc.vector.tensor_copy(
+            out=w_dealt[:].rearrange("p (t m) -> p t m", t=PACK),
+            in_=w_raw[:].bitcast(U16).rearrange("p (m t) -> p t m", t=PACK),
+        )
+        nc.vector.tensor_copy(
+            out=w_plane[:].rearrange("p (t m) -> p t m", t=PACK),
+            in_=w_plane_raw[:].rearrange("p (m t) -> p t m", t=PACK),
+        )
+        x_short_plane = keep.tile([P, J], U8, name="x_short_plane", align_bytes=64)
+        nc.vector.tensor_copy(x_short_plane[:], x_plane[:].indirect(idx4[:]))
+        x_picked = keep.tile([P, J], U32, name="x_picked", align_bytes=64)
+        nc.vector.tensor_copy(x_picked[:], x_words[:].bitcast(U32).indirect(idx[:]))
+
+        first = [psum.tile([P, 2, J], F32, name=f"first{b}") for b in range(2)]
+        for t in range(PACK):
+            cols = slice(P * t, P * (t + 1))
+            nc.tensor.matmul_mx(
+                out=first[t // 2][:, t % 2, :],
+                lhsT=w_dealt[:, cols].bitcast(E2M1X4),
+                lhsT_scale=w_plane[:, cols],
+                rhs=x_picked[:].bitcast(E5M2X4),
+                rhs_scale=x_picked_plane[:],
+                start=True,
+                stop=True,
+            )
+
+        x_short = keep.tile([P, J], U32, name="x_short", align_bytes=64)
+        nc.vector.tensor_copy(x_short[:], x_words[:].bitcast(U32).indirect(idx4[:]))
+        for q in range(QUADS):
+            rows = slice(QUAD * q, QUAD * q + ROWS)
+            nc.vector.tensor_copy(
+                out=out_plane[rows, :].bitcast(I32).rearrange("r (m c) -> r m c", m=2), in_=out_staged[:, :, q, :]
+            )
+
+        result = [[psum.tile([P, HALF], F32, name=f"result{s}{h}") for h in range(2)] for s in range(2)]
+        for s in range(2):
+            slots = slice(HALF * s, HALF * (s + 1))
+            for h in range(2):
+                nc.tensor.matmul_mx(
+                    out=result[s][h][:],
+                    lhsT=ws_codes[:, 2 * P * h : 2 * P * (h + 1)].bitcast(E2M1X4),
+                    lhsT_scale=out_plane[:, P * h : P * (h + 1)],
+                    rhs=x_short[:, slots].bitcast(E5M2X4),
+                    rhs_scale=x_short_plane[:, slots],
+                    start=True,
+                    stop=False,
+                )
+
+        upper = keep.tile([P, PACK, J], F32, name="upper")
+        lower = keep.tile([P, PACK, J], F32, name="lower")
+        cut = keep.tile([P, PACK, J], F32, name="cut")
+
+        def bounds(t, s0, s1):
+            slots = slice(s0, s1)
+            entries = slice(s0 // 16, s1 // 16)
+            nc.scalar.activation(
+                out=upper[:, t, slots], in_=table[t][:].indirect(idx2[:, entries]), func=COPY, scale=upper_step[:, t : t + 1]
+            )
+            nc.vector.tensor_tensor(out=cut[:, t, slots], in0=first[t // 2][:, t % 2, slots], in1=upper[:, t, slots], op=MIN)
+            nc.scalar.activation(
+                out=lower[:, t, slots], in_=table[t][:].indirect(idx3[:, entries]), func=COPY, scale=lower_step[:, t : t + 1]
+            )
+
+        for t in range(PACK - 1):
+            bounds(t, 0, J)
+
+        out_rows = out.rearrange("(h p) j -> p h j", p=P)
+        for s in range(2):
+            slots = slice(HALF * s, HALF * (s + 1))
+            bounds(PACK - 1, HALF * s, HALF * (s + 1))
+            hid = keep.tile([P, HALF * PACK], BF16, name=f"hid{s}", align_bytes=64)
+            nc.vector.tensor_tensor(
+                out=hid[:].rearrange("p (c i t) -> p c t i", i=4, t=PACK),
+                in0=cut[:, :, slots].rearrange("p t (c i) -> p c t i", i=4),
+                in1=lower[:, :, slots].rearrange("p t (c i) -> p c t i", i=4),
+                op=MAX,
+            )
+            hid_codes = keep.tile([P, HALF], U32, name=f"hid_codes{s}", align_bytes=64)
+            hid_plane = keep.tile([P, HALF], U8, name=f"hid_plane{s}", align_bytes=64)
+            nc.vector.quantize_mx(out=hid_codes[:].bitcast(E4M3X4), scales=hid_plane[:], in_=hid[:])
+            for h in range(2):
+                nc.tensor.matmul_mx(
+                    out=result[s][h][:],
+                    lhsT=wb_codes[:, 2 * P * h : 2 * P * (h + 1)].bitcast(E2M1X4),
+                    lhsT_scale=out_plane[:, N + P * h : N + P * (h + 1)],
+                    rhs=hid_codes[:].bitcast(E4M3X4),
+                    rhs_scale=hid_plane[:],
+                    start=False,
+                    stop=True,
+                )
+            for h in range(2):
+                staged = keep.tile([P, HALF], F32, name=f"staged{s}{h}")
+                if s == 1 and h == 1:
+                    nc.vector.tensor_copy(out=staged[:], in_=result[s][h][:])
+                else:
+                    nc.scalar.copy(out=staged[:], in_=result[s][h][:])
+                queue = nc.scalar if (s == 1 and h == 0) else nc.sync
+                queue.dma_start(out=out_rows[:, h, slots], in_=staged[:])

@@ -25,6 +25,12 @@ QUAD = 32
 ROWS = 4
 HALF = J // 2
 LIST_COLS = J // 16
+HOME = 2
+WEIGHT_COLS = R + 2 * N
+
+
+def quadrant(q, rows=QUAD):
+    return slice(QUAD * q, QUAD * q + rows)
 
 
 def load_scale_rows(queue, staged, scales):
@@ -51,58 +57,53 @@ def tile_list_twostepbounds_solo_further_plain_kernel(
         x_staged = keep.tile([ROWS, QUADS, T // 4], I32, name="x_staged")
         x_plane = keep.tile([P, T], U8, name="x_plane", align_bytes=64)
         w_raw = keep.tile([P, R // 2], I32, name="w_raw", align_bytes=64)
-        w_staged = keep.tile([ROWS, QUADS, R // 4], I32, name="w_staged")
-        w_plane_raw = keep.tile([P, R], U8, name="w_plane_raw", align_bytes=64)
         w_dealt = keep.tile([P, R], U16, name="w_dealt", align_bytes=64)
         w_plane = keep.tile([P, R], U8, name="w_plane", align_bytes=64)
         ws_codes = keep.tile([P, 2 * N], U8, name="ws_codes", align_bytes=64)
         wb_codes = keep.tile([P, 2 * N], U8, name="wb_codes", align_bytes=64)
-        out_staged = keep.tile([ROWS, 2, QUADS, N // 4], I32, name="out_staged")
-        out_plane = keep.tile([P, 2 * N], U8, name="out_plane", align_bytes=64)
+        weight_scales = keep.tile([P, QUADS, WEIGHT_COLS // 4], I32, name="weight_scales", align_bytes=64)
+        weight_plane = weight_scales[:, HOME, :].bitcast(U8)
+        home_rows = weight_scales[quadrant(HOME, ROWS), :, :]
 
         tb_planes = tb.rearrange("(p t) v -> p t v", t=PACK)
 
+        nc.vector.memset(weight_scales[quadrant(HOME), :, :], 0)
+        nc.vector.memset(x_plane[:].bitcast(I32), 0)
+
+        nc.gpsimd.dma_start(out=lower_step[:], in_=sb.rearrange("(p t) o -> p (t o)", t=PACK))
         nc.sync.dma_start(idx2[:], offs2)
         nc.sync.dma_start(out=upper_step[:], in_=sa.rearrange("(p t) o -> p (t o)", t=PACK))
-        nc.sync.dma_start(out=table[0][:], in_=tb_planes[:, 0, :])
         load_scale_rows(nc.sync, x_staged[:], xt_scales)
-        nc.sync.dma_start(idx3[:], offs3)
-        nc.sync.dma_start(out=lower_step[:], in_=sb.rearrange("(p t) o -> p (t o)", t=PACK))
         nc.sync.dma_start(idx[:], offs)
+        nc.sync.dma_start(out=table[0][:], in_=tb_planes[:, 0, :])
+        nc.sync.dma_start(idx3[:], offs3)
+        load_scale_rows(nc.sync, home_rows[:, :, 0 : R // 4], w_scales)
         nc.sync.dma_start(out=table[1][:], in_=tb_planes[:, 1, :])
-        load_scale_rows(nc.sync, w_staged[:], w_scales)
-        nc.sync.dma_start(out=x_words[:], in_=xt_words[0].rearrange("p c r -> p (c r)").bitcast(I32))
+        load_scale_rows(nc.sync, home_rows[:, :, R // 4 : (R + N) // 4], ws_scales)
+        load_scale_rows(nc.sync, home_rows[:, :, (R + N) // 4 :], wb_scales)
         nc.sync.dma_start(out=w_raw[:], in_=w_words[0].bitcast(I32))
+        nc.sync.dma_start(out=x_words[:], in_=xt_words[0].rearrange("p c r -> p (c r)").bitcast(I32))
         nc.sync.dma_start(idx4[:], offs4)
         nc.sync.dma_start(out=table[2][:], in_=tb_planes[:, 2, :])
-        load_scale_rows(nc.sync, out_staged[:, 0, :, :], ws_scales)
-        load_scale_rows(nc.sync, out_staged[:, 1, :, :], wb_scales)
         nc.sync.dma_start(out=table[3][:], in_=tb_planes[:, 3, :])
         nc.sync.dma_start(out=ws_codes[:].bitcast(I32), in_=ws_words[0].bitcast(I32))
         nc.sync.dma_start(out=wb_codes[:].bitcast(I32), in_=wb_words[0].bitcast(I32))
 
-        nc.vector.memset(x_plane[:].bitcast(I32), 0)
-        nc.vector.memset(w_plane_raw[:].bitcast(I32), 0)
-        nc.vector.memset(out_plane[:].bitcast(I32), 0)
         for q in range(QUADS):
-            rows = slice(QUAD * q, QUAD * q + ROWS)
-            nc.vector.tensor_copy(out=x_plane[rows, :].bitcast(I32), in_=x_staged[:, q, :])
-        for q in range(QUADS):
-            rows = slice(QUAD * q, QUAD * q + ROWS)
-            nc.vector.tensor_copy(out=w_plane_raw[rows, :].bitcast(I32), in_=w_staged[:, q, :])
-
+            nc.vector.tensor_copy(out=x_plane[quadrant(q, ROWS), :].bitcast(I32), in_=x_staged[:, q, :])
         x_picked_plane = keep.tile([P, J], U8, name="x_picked_plane", align_bytes=64)
         nc.vector.tensor_copy(x_picked_plane[:], x_plane[:].indirect(idx[:]))
+        for q in range(QUADS):
+            if q != HOME:
+                nc.vector.tensor_copy(out=weight_scales[quadrant(q), HOME, :], in_=weight_scales[quadrant(HOME), q, :])
+        nc.vector.tensor_copy(
+            out=w_plane[:].rearrange("p (t m) -> p t m", t=PACK),
+            in_=weight_plane[:, 0:R].rearrange("p (m t) -> p t m", t=PACK),
+        )
         nc.vector.tensor_copy(
             out=w_dealt[:].rearrange("p (t m) -> p t m", t=PACK),
             in_=w_raw[:].bitcast(U16).rearrange("p (m t) -> p t m", t=PACK),
         )
-        nc.vector.tensor_copy(
-            out=w_plane[:].rearrange("p (t m) -> p t m", t=PACK),
-            in_=w_plane_raw[:].rearrange("p (m t) -> p t m", t=PACK),
-        )
-        x_short_plane = keep.tile([P, J], U8, name="x_short_plane", align_bytes=64)
-        nc.vector.tensor_copy(x_short_plane[:], x_plane[:].indirect(idx4[:]))
         x_picked = keep.tile([P, J], U32, name="x_picked", align_bytes=64)
         nc.vector.tensor_copy(x_picked[:], x_words[:].bitcast(U32).indirect(idx[:]))
 
@@ -119,13 +120,10 @@ def tile_list_twostepbounds_solo_further_plain_kernel(
                 stop=True,
             )
 
+        x_short_plane = keep.tile([P, J], U8, name="x_short_plane", align_bytes=64)
+        nc.vector.tensor_copy(x_short_plane[:], x_plane[:].indirect(idx4[:]))
         x_short = keep.tile([P, J], U32, name="x_short", align_bytes=64)
         nc.vector.tensor_copy(x_short[:], x_words[:].bitcast(U32).indirect(idx4[:]))
-        for q in range(QUADS):
-            rows = slice(QUAD * q, QUAD * q + ROWS)
-            nc.vector.tensor_copy(
-                out=out_plane[rows, :].bitcast(I32).rearrange("r (m c) -> r m c", m=2), in_=out_staged[:, :, q, :]
-            )
 
         result = [[psum.tile([P, HALF], F32, name=f"result{s}{h}") for h in range(2)] for s in range(2)]
         for s in range(2):
@@ -134,7 +132,7 @@ def tile_list_twostepbounds_solo_further_plain_kernel(
                 nc.tensor.matmul_mx(
                     out=result[s][h][:],
                     lhsT=ws_codes[:, 2 * P * h : 2 * P * (h + 1)].bitcast(E2M1X4),
-                    lhsT_scale=out_plane[:, P * h : P * (h + 1)],
+                    lhsT_scale=weight_plane[:, R + P * h : R + P * (h + 1)],
                     rhs=x_short[:, slots].bitcast(E5M2X4),
                     rhs_scale=x_short_plane[:, slots],
                     start=True,
@@ -145,29 +143,33 @@ def tile_list_twostepbounds_solo_further_plain_kernel(
         lower = keep.tile([P, PACK, J], F32, name="lower")
         cut = keep.tile([P, PACK, J], F32, name="cut")
 
-        def bounds(t, s0, s1):
-            slots = slice(s0, s1)
-            entries = slice(s0 // 16, s1 // 16)
+        def fetch(bound, entries, step, t, slots):
             nc.scalar.activation(
-                out=upper[:, t, slots], in_=table[t][:].indirect(idx2[:, entries]), func=COPY, scale=upper_step[:, t : t + 1]
-            )
-            nc.vector.tensor_tensor(out=cut[:, t, slots], in0=first[t // 2][:, t % 2, slots], in1=upper[:, t, slots], op=MIN)
-            nc.scalar.activation(
-                out=lower[:, t, slots], in_=table[t][:].indirect(idx3[:, entries]), func=COPY, scale=lower_step[:, t : t + 1]
+                out=bound[:, t, slots],
+                in_=table[t][:].indirect(entries[:, slots.start // 16 : slots.stop // 16]),
+                func=COPY,
+                scale=step[:, t : t + 1],
             )
 
+        every = slice(0, J)
         for t in range(PACK - 1):
-            bounds(t, 0, J)
+            fetch(upper, idx2, upper_step, t, every)
+            fetch(lower, idx3, lower_step, t, every)
+        nc.vector.tensor_tensor(out=cut[:, 0:2, :], in0=first[0][:], in1=upper[:, 0:2, :], op=MIN)
+        nc.vector.tensor_tensor(out=cut[:, 2, :], in0=first[1][:, 0, :], in1=upper[:, 2, :], op=MIN)
 
         out_rows = out.rearrange("(h p) j -> p h j", p=P)
+        last = PACK - 1
         for s in range(2):
             slots = slice(HALF * s, HALF * (s + 1))
-            bounds(PACK - 1, HALF * s, HALF * (s + 1))
+            fetch(upper, idx2, upper_step, last, slots)
+            fetch(lower, idx3, lower_step, last, slots)
+            nc.vector.tensor_tensor(out=cut[:, last, slots], in0=first[1][:, 1, slots], in1=upper[:, last, slots], op=MIN)
             hid = keep.tile([P, HALF * PACK], BF16, name=f"hid{s}", align_bytes=64)
             nc.vector.tensor_tensor(
-                out=hid[:].rearrange("p (c i t) -> p c t i", i=4, t=PACK),
-                in0=cut[:, :, slots].rearrange("p t (c i) -> p c t i", i=4),
-                in1=lower[:, :, slots].rearrange("p t (c i) -> p c t i", i=4),
+                out=hid[:].rearrange("p (c i t) -> p c t i", i=2, t=PACK),
+                in0=cut[:, :, slots].rearrange("p t (c i) -> p c t i", i=2),
+                in1=lower[:, :, slots].rearrange("p t (c i) -> p c t i", i=2),
                 op=MAX,
             )
             hid_codes = keep.tile([P, HALF], U32, name=f"hid_codes{s}", align_bytes=64)
@@ -177,7 +179,7 @@ def tile_list_twostepbounds_solo_further_plain_kernel(
                 nc.tensor.matmul_mx(
                     out=result[s][h][:],
                     lhsT=wb_codes[:, 2 * P * h : 2 * P * (h + 1)].bitcast(E2M1X4),
-                    lhsT_scale=out_plane[:, N + P * h : N + P * (h + 1)],
+                    lhsT_scale=weight_plane[:, R + N + P * h : R + N + P * (h + 1)],
                     rhs=hid_codes[:].bitcast(E4M3X4),
                     rhs_scale=hid_plane[:],
                     start=False,

from contextlib import ExitStack

import concourse.mybir as mybir

K, T, J, R, V, N = 512, 1024, 256, 512, 1024, 256
FLOPS = 2 * K * R * J + 2 * R * N * J + 2 * K * N * J

F32 = mybir.dt.float32
BF16 = mybir.dt.bfloat16
I32 = mybir.dt.int32
U32 = mybir.dt.uint32
U16 = mybir.dt.uint16
U8 = mybir.dt.uint8
E4M3X4 = mybir.dt.float8_e4m3fn_x4
E5M2X4 = mybir.dt.float8_e5m2_x4
E2M1X4 = mybir.dt.float4_e2m1fn_x4
COPY = mybir.ActivationFunctionType.Copy
MIN = mybir.AluOpType.min
MAX = mybir.AluOpType.max

P = 128
PACK = 4
QUADS = 4
QUAD = 32
ROWS = 4
HALF = J // 2
LIST_COLS = J // 16
HOME = 2
WEIGHT_COLS = R + 2 * N


def quadrant(q, rows=QUAD):
    return slice(QUAD * q, QUAD * q + rows)


def load_scale_rows(queue, staged, scales):
    queue.dma_start(out=staged, in_=scales[0].rearrange("(q r) c -> r q c", r=ROWS).bitcast(I32))


def tile_list_twostepbounds_solo_further_plain_kernel(
    tc, xt_words, xt_scales, w_words, w_scales, tb, sa, sb, wb_words, wb_scales, ws_words, ws_scales,
    offs, offs2, offs3, offs4, out,
):
    nc = tc.nc
    with ExitStack() as ctx:
        keep = ctx.enter_context(tc.tile_pool(name="keep", bufs=1))
        psum = ctx.enter_context(tc.psum_pool(name="psum", bufs=1))

        idx = keep.tile([P, LIST_COLS], U16, name="idx")
        idx2 = keep.tile([P, LIST_COLS], U16, name="idx2")
        idx3 = keep.tile([P, LIST_COLS], U16, name="idx3")
        idx4 = keep.tile([P, LIST_COLS], U16, name="idx4")
        table = [keep.tile([P, V], F32, name=f"table{t}", align_bytes=64) for t in range(PACK)]
        upper_step = keep.tile([P, PACK], F32, name="upper_step")
        lower_step = keep.tile([P, PACK], F32, name="lower_step")
        x_words = keep.tile([P, T], I32, name="x_words", align_bytes=64)
        x_staged = keep.tile([ROWS, QUADS, T // 4], I32, name="x_staged")
        x_plane = keep.tile([P, T], U8, name="x_plane", align_bytes=64)
        w_raw = keep.tile([P, R // 2], I32, name="w_raw", align_bytes=64)
        w_dealt = keep.tile([P, R], U16, name="w_dealt", align_bytes=64)
        w_plane = keep.tile([P, R], U8, name="w_plane", align_bytes=64)
        ws_codes = keep.tile([P, 2 * N], U8, name="ws_codes", align_bytes=64)
        wb_codes = keep.tile([P, 2 * N], U8, name="wb_codes", align_bytes=64)
        weight_scales = keep.tile([P, QUADS, WEIGHT_COLS // 4], I32, name="weight_scales", align_bytes=64)
        weight_plane = weight_scales[:, HOME, :].bitcast(U8)
        home_rows = weight_scales[quadrant(HOME, ROWS), :, :]

        tb_planes = tb.rearrange("(p t) v -> p t v", t=PACK)

        nc.vector.memset(weight_scales[quadrant(HOME), :, :], 0)
        nc.vector.memset(x_plane[:].bitcast(I32), 0)

        nc.gpsimd.dma_start(out=lower_step[:], in_=sb.rearrange("(p t) o -> p (t o)", t=PACK))
        nc.sync.dma_start(idx2[:], offs2)
        nc.sync.dma_start(out=upper_step[:], in_=sa.rearrange("(p t) o -> p (t o)", t=PACK))
        load_scale_rows(nc.sync, x_staged[:], xt_scales)
        nc.sync.dma_start(idx[:], offs)
        nc.sync.dma_start(out=table[0][:], in_=tb_planes[:, 0, :])
        nc.sync.dma_start(idx3[:], offs3)
        load_scale_rows(nc.sync, home_rows[:, :, 0 : R // 4], w_scales)
        nc.sync.dma_start(out=table[1][:], in_=tb_planes[:, 1, :])
        load_scale_rows(nc.sync, home_rows[:, :, R // 4 : (R + N) // 4], ws_scales)
        load_scale_rows(nc.sync, home_rows[:, :, (R + N) // 4 :], wb_scales)
        nc.sync.dma_start(out=w_raw[:], in_=w_words[0].bitcast(I32))
        nc.sync.dma_start(out=x_words[:], in_=xt_words[0].rearrange("p c r -> p (c r)").bitcast(I32))
        nc.sync.dma_start(idx4[:], offs4)
        nc.sync.dma_start(out=table[2][:], in_=tb_planes[:, 2, :])
        nc.sync.dma_start(out=table[3][:], in_=tb_planes[:, 3, :])
        nc.sync.dma_start(out=ws_codes[:].bitcast(I32), in_=ws_words[0].bitcast(I32))
        nc.sync.dma_start(out=wb_codes[:].bitcast(I32), in_=wb_words[0].bitcast(I32))

        for q in range(QUADS):
            nc.vector.tensor_copy(out=x_plane[quadrant(q, ROWS), :].bitcast(I32), in_=x_staged[:, q, :])
        x_picked_plane = keep.tile([P, J], U8, name="x_picked_plane", align_bytes=64)
        nc.vector.tensor_copy(x_picked_plane[:], x_plane[:].indirect(idx[:]))
        for q in range(QUADS):
            if q != HOME:
                nc.vector.tensor_copy(out=weight_scales[quadrant(q), HOME, :], in_=weight_scales[quadrant(HOME), q, :])
        nc.vector.tensor_copy(
            out=w_plane[:].rearrange("p (t m) -> p t m", t=PACK),
            in_=weight_plane[:, 0:R].rearrange("p (m t) -> p t m", t=PACK),
        )
        nc.vector.tensor_copy(
            out=w_dealt[:].rearrange("p (t m) -> p t m", t=PACK),
            in_=w_raw[:].bitcast(U16).rearrange("p (m t) -> p t m", t=PACK),
        )
        x_picked = keep.tile([P, J], U32, name="x_picked", align_bytes=64)
        nc.vector.tensor_copy(x_picked[:], x_words[:].bitcast(U32).indirect(idx[:]))

        first = [psum.tile([P, 2, J], F32, name=f"first{b}") for b in range(2)]
        for t in range(PACK):
            cols = slice(P * t, P * (t + 1))
            nc.tensor.matmul_mx(
                out=first[t // 2][:, t % 2, :],
                lhsT=w_dealt[:, cols].bitcast(E2M1X4),
                lhsT_scale=w_plane[:, cols],
                rhs=x_picked[:].bitcast(E5M2X4),
                rhs_scale=x_picked_plane[:],
                start=True,
                stop=True,
            )

        x_short_plane = keep.tile([P, J], U8, name="x_short_plane", align_bytes=64)
        nc.vector.tensor_copy(x_short_plane[:], x_plane[:].indirect(idx4[:]))
        x_short = keep.tile([P, J], U32, name="x_short", align_bytes=64)
        nc.vector.tensor_copy(x_short[:], x_words[:].bitcast(U32).indirect(idx4[:]))

        result = [[psum.tile([P, HALF], F32, name=f"result{s}{h}") for h in range(2)] for s in range(2)]
        for s in range(2):
            slots = slice(HALF * s, HALF * (s + 1))
            for h in range(2):
                nc.tensor.matmul_mx(
                    out=result[s][h][:],
                    lhsT=ws_codes[:, 2 * P * h : 2 * P * (h + 1)].bitcast(E2M1X4),
                    lhsT_scale=weight_plane[:, R + P * h : R + P * (h + 1)],
                    rhs=x_short[:, slots].bitcast(E5M2X4),
                    rhs_scale=x_short_plane[:, slots],
                    start=True,
                    stop=False,
                )

        upper = keep.tile([P, PACK, J], F32, name="upper")
        lower = keep.tile([P, PACK, J], F32, name="lower")
        cut = keep.tile([P, PACK, J], F32, name="cut")

        def fetch(bound, entries, step, t, slots):
            nc.scalar.activation(
                out=bound[:, t, slots],
                in_=table[t][:].indirect(entries[:, slots.start // 16 : slots.stop // 16]),
                func=COPY,
                scale=step[:, t : t + 1],
            )

        every = slice(0, J)
        for t in range(PACK - 1):
            fetch(upper, idx2, upper_step, t, every)
            fetch(lower, idx3, lower_step, t, every)
        nc.vector.tensor_tensor(out=cut[:, 0:2, :], in0=first[0][:], in1=upper[:, 0:2, :], op=MIN)
        nc.vector.tensor_tensor(out=cut[:, 2, :], in0=first[1][:, 0, :], in1=upper[:, 2, :], op=MIN)

        out_rows = out.rearrange("(h p) j -> p h j", p=P)
        last = PACK - 1
        for s in range(2):
            slots = slice(HALF * s, HALF * (s + 1))
            fetch(upper, idx2, upper_step, last, slots)
            fetch(lower, idx3, lower_step, last, slots)
            nc.vector.tensor_tensor(out=cut[:, last, slots], in0=first[1][:, 1, slots], in1=upper[:, last, slots], op=MIN)
            hid = keep.tile([P, HALF * PACK], BF16, name=f"hid{s}", align_bytes=64)
            nc.vector.tensor_tensor(
                out=hid[:].rearrange("p (c i t) -> p c t i", i=2, t=PACK),
                in0=cut[:, :, slots].rearrange("p t (c i) -> p c t i", i=2),
                in1=lower[:, :, slots].rearrange("p t (c i) -> p c t i", i=2),
                op=MAX,
            )
            hid_codes = keep.tile([P, HALF], U32, name=f"hid_codes{s}", align_bytes=64)
            hid_plane = keep.tile([P, HALF], U8, name=f"hid_plane{s}", align_bytes=64)
            nc.vector.quantize_mx(out=hid_codes[:].bitcast(E4M3X4), scales=hid_plane[:], in_=hid[:])
            for h in range(2):
                nc.tensor.matmul_mx(
                    out=result[s][h][:],
                    lhsT=wb_codes[:, 2 * P * h : 2 * P * (h + 1)].bitcast(E2M1X4),
                    lhsT_scale=weight_plane[:, R + N + P * h : R + N + P * (h + 1)],
                    rhs=hid_codes[:].bitcast(E4M3X4),
                    rhs_scale=hid_plane[:],
                    start=False,
                    stop=True,
                )
            for h in range(2):
                staged = keep.tile([P, HALF], F32, name=f"staged{s}{h}")
                if s == 1 and h == 1:
                    nc.vector.tensor_copy(out=staged[:], in_=result[s][h][:])
                else:
                    nc.scalar.copy(out=staged[:], in_=result[s][h][:])
                queue = nc.scalar if (s == 1 and h == 0) else nc.sync
                queue.dma_start(out=out_rows[:, h, slots], in_=staged[:])
